import numpy as np, ml_dtypes
CORES = [10,34,74,98]
N = 4
import mx_ref
BF = ml_dtypes.bfloat16
def entries(a):
    return np.ascontiguousarray(a.T).reshape(-1)
def table(e):
    return np.ascontiguousarray(np.reshape(e, (-1, 16)).T).astype(np.int32)
def cols(t, e):
    v = np.concatenate([t.reshape(128, -1, 4), np.zeros((128, 1, 4), BF)], axis=1)
    return np.ascontiguousarray(v[:, e]).reshape(128, -1)
def tile(rs):
    return np.stack(rs, axis=2).reshape(128, -1).astype(BF)
def cut(t, i, w=512):
    return t[:, w * i:w * i + w]
def f(rng, *shape):
    return mx_ref.flush((rng.standard_normal(shape, dtype=np.float32) * np.exp2(rng.integers(-2, 3, shape[:-1] + (1,)))).astype(BF))
def wide(rng, *shape, cols=0):
    v = rng.standard_normal(shape, dtype=np.float32) * np.exp2(rng.integers(-12, 13, shape)).astype(np.float32)
    if cols: v *= np.repeat(np.exp2(rng.integers(-cols, cols + 1, shape[:-2] + (1, shape[-1] // 4))) * (rng.random(shape[:-2] + (1, shape[-1] // 4)) > 0.0625), 4, axis=-1).astype(np.float32)
    return mx_ref.flush(v.astype(BF))
T, P, CAPP = 256, 128, 32
BASE = T + 3 * P
def sends(a):
    return entries(a).reshape(3, N, CAPP)
def filled(s, r, t):
    return s[:, :t, r].transpose(1, 0, 2).reshape(-1) >= 0
def lists(rng, how=""):
    s = np.full((N, 3, N, CAPP), -1)
    a = int(rng.integers(0, N)); same = (a, int(rng.integers(0, 3)), (a + int(rng.integers(1, N))) % N)
    for t in range(3):
        for q in range(N):
            got = BASE + np.flatnonzero(filled(s, q, t))
            for r in range(N):
                if q == r: continue
                least = 1 if t == 0 and r == (q + 1) % N else 0
                k = rng.permutation(CAPP)[:CAPP if how == "far" else rng.integers(least, CAPP + 1)]
                e = rng.integers(T + (t - 1) * P if how == "far" and t > 0 else 0, T + t * P, len(k))
                if t > 0:
                    m = (len(k) + 1) // 2; e[:m] = got[rng.integers(0, len(got), m)]
                s[q, t, r, k] = e
                if how == "shared" and (q, t, r) == same: s[q, t, r] = rng.integers(0, T + t * P)
    c = np.zeros((N, 2, 3, P), int)
    for r in range(N):
        for t in range(3):
            low = 2 if how == "skip" and t == 2 else t + 1
            own = T + (low - 1) * P; got = BASE + np.flatnonzero(filled(s, r, low))
            for h in range(2):
                c[r, h, t] = rng.integers(0, own, P)
                if len(got):
                    there = np.ones(P, bool) if how == "far" else rng.random(P) < 0.5
                    c[r, h, t] = np.where(there, got[rng.integers(0, len(got), P)], c[r, h, t])
            if how == "shared":
                one = int(c[r, 0, t, 0]); k = rng.permutation(P)
                c[r, 0, t, k[:P - P // 8]] = one; c[r, 1, t, k[:P // 8]] = one
            if how == "chains":
                c[r, 0, t] = np.arange(P) % T if t == 0 else T + (t - 1) * P + np.arange(P)
                c[r, 1, t] = rng.integers(0, T, P)
    return {"sn": np.stack([table(s[r]) for r in range(N)]), "lc": np.stack([table(c[r, 0]) for r in range(N)]), "rc": np.stack([table(c[r, 1]) for r in range(N)])}
def setup_inputs(rng):
    return {"x": f(rng, N, 128, 4 * T), "wl": np.stack([f(rng, 128, 2048)] * N), "wr": np.stack([f(rng, 128, 2048)] * N), "v": f(rng, N, 128, 512), **lists(rng)}
def setup_inputs_chains(rng):
    return {**setup_inputs(rng), **lists(rng, "chains")}
def setup_inputs_far(rng):
    return {**setup_inputs(rng), **lists(rng, "far")}
def setup_inputs_shared(rng):
    return {**setup_inputs(rng), **lists(rng, "shared")}
def setup_inputs_skip(rng):
    return {**setup_inputs(rng), **lists(rng, "skip")}
def setup_inputs_spread(rng):
    d = setup_inputs(rng); d["x"] = wide(rng, N, 128, 4 * T, cols=8); return d
def check_inputs(d):
    b = []
    for n in ("wl", "wr"):
        if any((d[n][r] != d[n][0]).any() for r in range(N)): b.append(n)
    s = np.stack([sends(d["sn"][r]) for r in range(N)])
    for r in range(N):
        for t in range(3):
            own = np.concatenate([np.ones(T + t * P, bool), np.zeros((3 - t) * P, bool)])
            ok = np.concatenate([own, filled(s, r, t)]); e = s[r, t]
            if e.min() < -1 or e.max() >= len(ok) or not ok[e[e >= 0]].all() or (s[r, t, r] != -1).any(): b.append("sn")
            ok = np.concatenate([own, filled(s, r, t + 1)])
            for n in ("lc", "rc"):
                e = entries(d[n][r])[t * P:t * P + P]
                if e.min() < 0 or e.max() >= len(ok) or not ok[e].all(): b.append(n)
    return b
def reference(x, wl, wr, v, sn, lc, rc):
    WL = [[mx_ref.quantize(np.ascontiguousarray(cut(wl[r], i))) for i in range(4)] for r in range(N)]
    WR = [[mx_ref.quantize(np.ascontiguousarray(cut(wr[r], i))) for i in range(4)] for r in range(N)]
    pool = [x[r] for r in range(N)]; slots = [[] for r in range(N)]
    for t in range(3):
        before = [np.concatenate([pool[r], np.zeros((128, 4 * (3 - t) * P), BF)] + slots[r], axis=1) for r in range(N)]
        for r in range(N):
            for q in range(N): slots[r].append(cols(before[q], sends(sn[q])[t, r]))
        made = []
        for r in range(N):
            known = np.concatenate([before[r]] + slots[r][t * N:], axis=1)
            left = mx_ref.quantize(cols(known, entries(lc[r])[t * P:t * P + P]))
            right = mx_ref.quantize(cols(known, entries(rc[r])[t * P:t * P + P]))
            made.append(tile([np.maximum(mx_ref.matmul(WL[r][i], left) + mx_ref.matmul(WR[r][i], right), np.float32(0)) * np.float32(0.05) for i in range(4)]))
        pool = [np.concatenate([pool[r], made[r]], axis=1) for r in range(N)]
    y = np.zeros((N, 128, P), np.float32)
    for r in range(N):
        y[r] = mx_ref.matmul(mx_ref.quantize(v[r]), mx_ref.quantize(np.ascontiguousarray(pool[r][:, 4 * (T + 2 * P):])))
    return {"y": y}

@@ -1,0 +1,247 @@
+from concourse.bass import DstId, RemoteDMATransfer
+from concourse.mybir import dt, AluOpType, ActivationFunctionType
+
+N, TL, P, CAPP = 4, 256, 128, 32
+BASE = TL + 3 * P
+KP = P // 16
+KS = CAPP // 16
+CODES, PLANE = "float8_e4m3fn_x4", "uint8"
+WIDE = [TL, BASE + N * CAPP, BASE + 2 * N * CAPP, BASE + 3 * N * CAPP]
+
+SCRATCH = {
+    "xt": ("sbuf", [128, 4 * TL], "bfloat16"),
+    "wlt": ("sbuf", [128, 2048], "bfloat16"),
+    "wrt": ("sbuf", [128, 2048], "bfloat16"),
+    "vt": ("sbuf", [128, 512], "bfloat16"),
+    "sni": ("sbuf", [128, 3 * N * KS], "int32"),
+    "lci": ("sbuf", [128, 3 * KP], "int32"),
+    "rci": ("sbuf", [128, 3 * KP], "int32"),
+    "lcu": ("sbuf", [128, 3 * KP], "uint16"),
+    "rcu": ("sbuf", [128, 3 * KP], "uint16"),
+    "wlc": ("sbuf", [128, 512], CODES), "wls": ("sbuf", [128, 512], PLANE),
+    "wrc": ("sbuf", [128, 512], CODES), "wrs": ("sbuf", [128, 512], PLANE),
+    "vc": ("sbuf", [128, 128], CODES), "vs": ("sbuf", [128, 128], PLANE),
+    "hc": ("sbuf", [128, P], CODES), "hs": ("sbuf", [128, P], PLANE),
+    "yt": ("sbuf", [128, P], "float32"),
+    "acc": ("psum", [128, 512 * 8], "float32"),
+}
+for _t in range(4):
+    SCRATCH["w%dc" % _t] = ("sbuf", [128, WIDE[_t]], CODES)
+    SCRATCH["w%ds" % _t] = ("sbuf", [128, WIDE[_t]], PLANE)
+for _t in (1, 2, 3):
+    SCRATCH["snu%d" % _t] = ("sbuf", [128, (N - 1) * KS], "uint16")
+    SCRATCH["out%dc" % _t] = ("sbuf", [128, (N - 1) * CAPP], CODES)
+    SCRATCH["out%ds" % _t] = ("sbuf", [128, (N - 1) * CAPP], PLANE)
+    SCRATCH["a%dc" % _t] = ("sbuf", [128, P], CODES)
+    SCRATCH["a%ds" % _t] = ("sbuf", [128, P], PLANE)
+    SCRATCH["b%dc" % _t] = ("sbuf", [128, P], CODES)
+    SCRATCH["b%ds" % _t] = ("sbuf", [128, P], PLANE)
+    SCRATCH["h%d" % _t] = ("sbuf", [128, 4 * P], "bfloat16")
+
+SEMAPHORES = ["ldx", "ldsn", "ldwl", "ldwr", "ldls", "ldv", "qx0", "ul", "qwl", "qwr", "qv", "qh", "ymm", "ycp", "yst",
+              "fill1", "fill2", "fill3", "cp12", "cp13", "cp23"]
+for _t in (1, 2, 3):
+    SEMAPHORES += ["%s%d" % (_n, _t) for _n in ("us", "pc", "ps", "goc", "gos", "arc", "ars", "alc", "als", "blc", "bls",
+                                               "ev", "qn", "m0x", "m1x", "m2x", "m3x")]
+
+
+def rank_program(g, core, T, topo):
+    me = T.rank_of(core)
+    if me is None:
+        return
+    S, V, A, PE, SY = T.sem, g.vector, g.scalar, g.tensor, g.sync
+    COPY, RELU = ActivationFunctionType.Copy, ActivationFunctionType.Relu
+
+    def receivers(s):
+        got = []
+        for j, (c0, c1, p0, p1) in enumerate(((0, 4, 0, 2), (4, 6, 2, 4), (6, 8, 4, 8))):
+            d = (s + 1 + j) % N
+            e = topo.engines(T.cores[s], T.cores[d])
+            k = len(e)
+            got.append((d, e[c0 * k // 8:c1 * k // 8], e[p0 * k // 8:p1 * k // 8]))
+        return got
+
+    def bits(engines):
+        m = 0
+        for e in engines:
+            m |= 1 << e
+        return m
+
+    need_c = sum(len(ec) for s in range(N) if s != me for d, ec, ep in receivers(s) if d == me)
+    need_p = sum(len(ep) for s in range(N) if s != me for d, ec, ep in receivers(s) if d == me)
+
+    def slot(t, s):
+        return BASE + ((t - 1) * N + s) * CAPP
+
+    runs = [(a, b) for a, b in ((0, me), (me + 1, N)) if a < b]
+
+    def load_list(q, dst, src, groups, sem):
+        for k in groups:
+            q.dma_start(dst[16 * k:16 * k + 16, :], src[:, :]).then_inc(sem, 16)
+
+    def quant(wc, ws, col, tile, n, sem):
+        return V.quantize_mx(T[wc][:, col:col + n], T[ws][:, col:col + n], tile[:, 0:4 * n]).then_inc(sem, 1)
+
+    def pick_codes(out, win, wide, off, e0, e1, sem):
+        V.tensor_copy(T[out][:, 0:16 * (e1 - e0)].bitcast(dt.uint32),
+                      T[win][:, 0:wide].bitcast(dt.uint32).indirect(off[:, e0:e1])).then_inc(sem, 1)
+
+    def pick_plane(out, win, wide, off, e0, e1, sem):
+        A.activation(T[out][:, 0:16 * (e1 - e0)], T[win][:, 0:wide].indirect(off[:, e0:e1]), COPY).then_inc(sem, 1)
+
+    def list_to_send(t):
+        c0 = (t - 1) * N * KS
+        first = (me + 1) % N
+        parts = [(first * KS, N * KS)] if first else []
+        if me:
+            parts.append((0, me * KS))
+        at = 0
+        for a, b in parts:
+            V.tensor_copy(T["snu%d" % t][:, at:at + b - a], T.sni[:, c0 + a:c0 + b]).then_inc(S["us%d" % t], 1)
+            at += b - a
+    n_us = 1 if me in (0, N - 1) else 2
+
+    def send(t):
+        for kind, width, ready, left, arrive in (("c", 4, "pc", "goc", "arc"), ("s", 1, "ps", "gos", "ars")):
+            g.wait_ge(S["%s%d" % (ready, t)], 1)
+            moves = []
+            for j, (d, ec, ep) in enumerate(receivers(me)):
+                rid, pid, _se = topo.addr(T.cores[d])
+                src = T["out%d%s" % (t, kind)][:, CAPP * j:CAPP * j + CAPP]
+                dst = T["w%d%s" % (t, kind)][:, slot(t, me):slot(t, me) + CAPP]
+                if kind == "c":
+                    src, dst = src.bitcast(dt.uint8), dst.bitcast(dt.uint8)
+                moves.append(RemoteDMATransfer(dst_ids=[DstId(rid=rid, pnc=pid)],
+                                               dma_engine_mask=bits(ec if kind == "c" else ep),
+                                               remote_sem=S["%s%d" % (arrive, t)], src=src, dst=dst))
+            g.remote_dma_fused(moves, local_sem=S["%s%d" % (left, t)])
+    sent_c = sum(len(ec) for d, ec, ep in receivers(me))
+    sent_p = sum(len(ep) for d, ec, ep in receivers(me))
+
+    def copy_slots(t, src, dst, sem):
+        for a, b in runs:
+            c0, c1 = slot(t, a), slot(t, b)
+            SY.dma_start(T["w%dc" % dst][:, c0:c1].bitcast(dt.uint8), T["w%dc" % src][:, c0:c1].bitcast(dt.uint8)).then_inc(S[sem], 16)
+            SY.dma_start(T["w%ds" % dst][:, c0:c1], T["w%ds" % src][:, c0:c1]).then_inc(S[sem], 16)
+    n_cp = 32 * len(runs)
+
+    def bank(t, i):
+        return 512 * (4 * ((t - 1) % 2) + i)
+
+    def scaled(q, t, i):
+        q.wait_ge(S["m%dx%d" % (i, t)], 1)
+        out, z = T["h%d" % t][:, i:4 * P:4], T.acc[:, bank(t, i):bank(t, i) + P]
+        if q is A:
+            A.activation(out, z, RELU, scale=0.05).then_inc(S["ev%d" % t], 1)
+        else:
+            V.tensor_scalar(out, z, 0.0, 0.05, AluOpType.max, AluOpType.mult).then_inc(S["ev%d" % t], 1)
+
+    n_fill = {1: 1, 2: 2, 3: 3}
+
+    def window_ready(q, t, arrived, need):
+        q.wait_ge(S["fill%d" % t], n_fill[t])
+        if t == 1:
+            q.wait_ge(S.ul, 2)
+        if t == 2:
+            q.wait_ge(S.cp12, n_cp)
+        if t == 3:
+            q.wait_ge(S.cp13, n_cp)
+            q.wait_ge(S.cp23, n_cp)
+        q.wait_ge(S["%s%d" % (arrived, t)], need)
+
+    SY.dma_start(T.xt[:, :], T.x[:, :]).then_inc(S.ldx, 16)
+    load_list(SY, T.sni, T.sn, range(0, 3), S.ldsn)
+    SY.dma_start(T.wlt[:, :], T.wl[:, :]).then_inc(S.ldwl, 16)
+    load_list(SY, T.lci, T.lc, range(8), S.ldls)
+    load_list(SY, T.rci, T.rc, range(8), S.ldls)
+    SY.wait_ge(S.arc1, need_c)
+    SY.wait_ge(S.ars1, need_p)
+    copy_slots(1, 1, 2, "cp12")
+    SY.wait_ge(S.goc2, sent_c)
+    SY.wait_ge(S.gos2, sent_p)
+    copy_slots(1, 1, 3, "cp13")
+    SY.dma_start(T.vt[:, :], T.v[:, :]).then_inc(S.ldv, 16)
+    SY.wait_ge(S.arc2, need_c)
+    SY.wait_ge(S.ars2, need_p)
+    copy_slots(2, 2, 3, "cp23")
+    SY.wait_ge(S.ycp, 1)
+    SY.dma_start(T.y[:, :], T.yt[:, :]).then_inc(S.yst, 16)
+    SY.wait_ge(S.yst, 16)
+
+    load_list(A, T.sni, T.sn, range(3, 8), S.ldsn)
+    A.dma_start(T.wrt[:, :], T.wr[:, :]).then_inc(S.ldwr, 16)
+    A.wait_ge(S.us1, n_us)
+    A.wait_ge(S.qx0, 1)
+    pick_plane("out1s", "w0s", WIDE[0], T.snu1, 0, (N - 1) * KS, S.ps1)
+    for t in (1, 2, 3):
+        window_ready(A, t, "ars", need_p)
+        pick_plane("a%ds" % t, "w%ds" % t, WIDE[t], T.lcu, KP * (t - 1), KP * t, S["als%d" % t])
+        pick_plane("b%ds" % t, "w%ds" % t, WIDE[t], T.rcu, KP * (t - 1), KP * t, S["bls%d" % t])
+        scaled(A, t, 0)
+        scaled(A, t, 2)
+        if t < 3:
+            A.wait_ge(S["us%d" % (t + 1)], n_us)
+            A.wait_ge(S["qn%d" % t], 1)
+            pick_plane("out%ds" % (t + 1), "w%ds" % t, WIDE[t], T["snu%d" % (t + 1)], 0, (N - 1) * KS, S["ps%d" % (t + 1)])
+
+    V.wait_ge(S.ldsn, 128)
+    list_to_send(1)
+    V.wait_ge(S.ldx, 16)
+    quant("w0c", "w0s", 0, T.xt, TL, S.qx0)
+    V.wait_ge(S.us1, n_us)
+    V.wait_ge(S.qx0, 1)
+    pick_codes("out1c", "w0c", WIDE[0], T.snu1, 0, (N - 1) * KS, S.pc1)
+    quant("w1c", "w1s", 0, T.xt, TL, S.fill1)
+    list_to_send(2)
+    list_to_send(3)
+    V.wait_ge(S.ldls, 256)
+    V.tensor_copy(T.lcu[:, :], T.lci[:, :]).then_inc(S.ul, 1)
+    V.tensor_copy(T.rcu[:, :], T.rci[:, :]).then_inc(S.ul, 1)
+    V.wait_ge(S.ldwl, 16)
+    quant("wlc", "wls", 0, T.wlt, 512, S.qwl)
+    V.wait_ge(S.ldwr, 16)
+    quant("wrc", "wrs", 0, T.wrt, 512, S.qwr)
+    for t in (1, 2, 3):
+        window_ready(V, t, "arc", need_c)
+        pick_codes("a%dc" % t, "w%dc" % t, WIDE[t], T.lcu, KP * (t - 1), KP * t, S["alc%d" % t])
+        pick_codes("b%dc" % t, "w%dc" % t, WIDE[t], T.rcu, KP * (t - 1), KP * t, S["blc%d" % t])
+        scaled(V, t, 1)
+        scaled(V, t, 3)
+        V.wait_ge(S["ev%d" % t], 4)
+        if t < 3:
+            quant("w%dc" % t, "w%ds" % t, TL + (t - 1) * P, T["h%d" % t], P, S["qn%d" % t])
+            V.wait_ge(S["us%d" % (t + 1)], n_us)
+            V.wait_ge(S["qn%d" % t], 1)
+            pick_codes("out%dc" % (t + 1), "w%dc" % t, WIDE[t], T["snu%d" % (t + 1)], 0, (N - 1) * KS, S["pc%d" % (t + 1)])
+            u = t + 1
+            quant("w%dc" % u, "w%ds" % u, 0, T.xt, TL, S["fill%d" % u])
+            for k in range(1, u):
+                quant("w%dc" % u, "w%ds" % u, TL + (k - 1) * P, T["h%d" % k], P, S["fill%d" % u])
+        else:
+            quant("hc", "hs", 0, T.h3, P, S.qh)
+        if t == 2:
+            V.wait_ge(S.ldv, 16)
+            quant("vc", "vs", 0, T.vt, 128, S.qv)
+    V.wait_ge(S.ymm, 1)
+    V.tensor_copy(T.yt[:, :], T.acc[:, bank(2, 0):bank(2, 0) + P]).then_inc(S.ycp, 1)
+
+    for t in (1, 2, 3):
+        for w, k, q in (("wl", "a", S.qwl), ("wr", "b", S.qwr)):
+            PE.wait_ge(q, 1)
+            PE.wait_ge(S["%slc%d" % (k, t)], 1)
+            PE.wait_ge(S["%sls%d" % (k, t)], 1)
+            for i in range(4):
+                m = PE.matmul_mx(T.acc[:, bank(t, i):bank(t, i) + P],
+                                 T[w + "c"][:, 128 * i:128 * i + 128], T[w + "s"][:, 128 * i:128 * i + 128],
+                                 T["%s%dc" % (k, t)][:, :], T["%s%ds" % (k, t)][:, :], k == "a", k == "b")
+                if k == "b":
+                    m.then_inc(S["m%dx%d" % (i, t)], 1)
+    PE.wait_ge(S.qv, 1)
+    PE.wait_ge(S.qh, 1)
+    PE.matmul_mx(T.acc[:, bank(2, 0):bank(2, 0) + P], T.vc[:, :], T.vs[:, :], T.hc[:, :], T.hs[:, :], True, True).then_inc(S.ymm, 1)
+
+    for t in (1, 2, 3):
+        send(t)
+    for t in (1, 2, 3):
+        g.wait_ge(S["goc%d" % t], sent_c)
+        g.wait_ge(S["gos%d" % t], sent_p)

@@ -1,4 +1,3 @@
-from concourse.bass import DstId, RemoteDMATransfer
 from concourse.mybir import dt, AluOpType, ActivationFunctionType
 
 N, TL, P, CAPP = 4, 256, 128, 32
@@ -7,6 +6,7 @@ KP = P // 16
 KS = CAPP // 16
 CODES, PLANE = "float8_e4m3fn_x4", "uint8"
 WIDE = [TL, BASE + N * CAPP, BASE + 2 * N * CAPP, BASE + 3 * N * CAPP]
+FIRST = {"c": ((0, 2), (2, 4), (4, 6)), "s": ((6, 8), (0, 4), (4, 8))}
 
 SCRATCH = {
     "xt": ("sbuf", [128, 4 * TL], "bfloat16"),
@@ -38,11 +38,11 @@ for _t in (1, 2, 3):
     SCRATCH["b%ds" % _t] = ("sbuf", [128, P], PLANE)
     SCRATCH["h%d" % _t] = ("sbuf", [128, 4 * P], "bfloat16")
 
-SEMAPHORES = ["ldx", "ldsn", "ldwl", "ldwr", "ldls", "ldv", "qx0", "ul", "qwl", "qwr", "qv", "qh", "ymm", "ycp", "yst",
-              "fill1", "fill2", "fill3", "cp12", "cp13", "cp23"]
+SEMAPHORES = ["ldx0", "ldx1", "ldsn", "ldwl", "ldwr", "ldls", "ldv", "qx0", "ul", "qwl", "qwr", "qv", "qh", "ymm", "ycp",
+              "yst", "fill1", "fill2", "fill3", "cp12", "cp13", "cp23"]
 for _t in (1, 2, 3):
-    SEMAPHORES += ["%s%d" % (_n, _t) for _n in ("us", "pc", "ps", "goc", "gos", "arc", "ars", "alc", "als", "blc", "bls",
-                                               "ev", "qn", "m0x", "m1x", "m2x", "m3x")]
+    SEMAPHORES += ["%s%d" % (_n, _t) for _n in ("us", "pcf", "pcr", "psf", "psr", "goc", "gos", "arc", "ars",
+                                               "alc", "als", "blc", "bls", "ev", "qn", "m0x", "m1x", "m2x", "m3x")]
 
 
 def rank_program(g, core, T, topo):
@@ -53,22 +53,20 @@ def rank_program(g, core, T, topo):
     COPY, RELU = ActivationFunctionType.Copy, ActivationFunctionType.Relu
 
     def receivers(s):
-        got = []
-        for j, (c0, c1, p0, p1) in enumerate(((0, 4, 0, 2), (4, 6, 2, 4), (6, 8, 4, 8))):
-            d = (s + 1 + j) % N
-            e = topo.engines(T.cores[s], T.cores[d])
-            k = len(e)
-            got.append((d, e[c0 * k // 8:c1 * k // 8], e[p0 * k // 8:p1 * k // 8]))
-        return got
+        return [(s + 1 + j) % N for j in range(N - 1)]
 
-    def bits(engines):
-        m = 0
-        for e in engines:
-            m |= 1 << e
-        return m
+    def lanes(s, d, t, kind):
+        e = topo.engines(T.cores[s], T.cores[d])
+        if t > 1:
+            return e
+        a, b = FIRST[kind][receivers(s).index(d)]
+        return e[a * len(e) // 8:b * len(e) // 8]
 
-    need_c = sum(len(ec) for s in range(N) if s != me for d, ec, ep in receivers(s) if d == me)
-    need_p = sum(len(ep) for s in range(N) if s != me for d, ec, ep in receivers(s) if d == me)
+    def need(t, kind):
+        return sum(len(lanes(s, me, t, kind)) for s in range(N) if s != me)
+
+    def sent(t, kind):
+        return sum(len(lanes(me, d, t, kind)) for d in receivers(me))
 
     def slot(t, s):
         return BASE + ((t - 1) * N + s) * CAPP
@@ -79,15 +77,19 @@ def rank_program(g, core, T, topo):
         for k in groups:
             q.dma_start(dst[16 * k:16 * k + 16, :], src[:, :]).then_inc(sem, 16)
 
-    def quant(wc, ws, col, tile, n, sem):
-        return V.quantize_mx(T[wc][:, col:col + n], T[ws][:, col:col + n], tile[:, 0:4 * n]).then_inc(sem, 1)
+    def quant(wc, ws, col, tile, n, sem, at=0):
+        V.quantize_mx(T[wc][:, col:col + n], T[ws][:, col:col + n], tile[:, 4 * at:4 * (at + n)]).then_inc(sem, 1)
 
-    def pick_codes(out, win, wide, off, e0, e1, sem):
-        V.tensor_copy(T[out][:, 0:16 * (e1 - e0)].bitcast(dt.uint32),
+    def pick_codes(out, win, wide, off, o0, e0, e1, sem):
+        V.tensor_copy(T[out][:, 16 * o0:16 * (o0 + e1 - e0)].bitcast(dt.uint32),
                       T[win][:, 0:wide].bitcast(dt.uint32).indirect(off[:, e0:e1])).then_inc(sem, 1)
 
-    def pick_plane(out, win, wide, off, e0, e1, sem):
-        A.activation(T[out][:, 0:16 * (e1 - e0)], T[win][:, 0:wide].indirect(off[:, e0:e1]), COPY).then_inc(sem, 1)
+    def pick_plane(q, out, win, wide, off, o0, e0, e1, sem):
+        dst, src = T[out][:, 16 * o0:16 * (o0 + e1 - e0)], T[win][:, 0:wide].indirect(off[:, e0:e1])
+        if q is A:
+            A.activation(dst, src, COPY).then_inc(sem, 1)
+        else:
+            V.tensor_copy(dst, src).then_inc(sem, 1)
 
     def list_to_send(t):
         c0 = (t - 1) * N * KS
@@ -101,22 +103,28 @@ def rank_program(g, core, T, topo):
             at += b - a
     n_us = 1 if me in (0, N - 1) else 2
 
+    def pick_to_send(q, t):
+        w, off = t - 1, T["snu%d" % t]
+        for e0, e1, f in ((0, KS, "f"), (KS, (N - 1) * KS, "r")):
+            if q is V:
+                pick_codes("out%dc" % t, "w%dc" % w, WIDE[w], off, e0, e0, e1, S["pc%s%d" % (f, t)])
+            else:
+                pick_plane(A, "out%ds" % t, "w%ds" % w, WIDE[w], off, e0, e0, e1, S["ps%s%d" % (f, t)])
+
     def send(t):
-        for kind, width, ready, left, arrive in (("c", 4, "pc", "goc", "arc"), ("s", 1, "ps", "gos", "ars")):
-            g.wait_ge(S["%s%d" % (ready, t)], 1)
-            moves = []
-            for j, (d, ec, ep) in enumerate(receivers(me)):
+        for kind, left, arrive in (("c", "goc", "arc"), ("s", "gos", "ars")):
+            for j, d in enumerate(receivers(me)):
+                if j < 2:
+                    g.wait_ge(S["p%s%s%d" % (kind, "fr"[j], t)], 1)
                 rid, pid, _se = topo.addr(T.cores[d])
                 src = T["out%d%s" % (t, kind)][:, CAPP * j:CAPP * j + CAPP]
                 dst = T["w%d%s" % (t, kind)][:, slot(t, me):slot(t, me) + CAPP]
                 if kind == "c":
                     src, dst = src.bitcast(dt.uint8), dst.bitcast(dt.uint8)
-                moves.append(RemoteDMATransfer(dst_ids=[DstId(rid=rid, pnc=pid)],
-                                               dma_engine_mask=bits(ec if kind == "c" else ep),
-                                               remote_sem=S["%s%d" % (arrive, t)], src=src, dst=dst))
-            g.remote_dma_fused(moves, local_sem=S["%s%d" % (left, t)])
-    sent_c = sum(len(ec) for d, ec, ep in receivers(me))
-    sent_p = sum(len(ep) for d, ec, ep in receivers(me))
+                mask = 0
+                for e in lanes(me, d, t, kind):
+                    mask |= 1 << e
+                g.remote_dma(dst, src, S["%s%d" % (arrive, t)], S["%s%d" % (left, t)], pid, rid, mask)
 
     def copy_slots(t, src, dst, sem):
         for a, b in runs:
@@ -136,10 +144,8 @@ def rank_program(g, core, T, topo):
         else:
             V.tensor_scalar(out, z, 0.0, 0.05, AluOpType.max, AluOpType.mult).then_inc(S["ev%d" % t], 1)
 
-    n_fill = {1: 1, 2: 2, 3: 3}
-
-    def window_ready(q, t, arrived, need):
-        q.wait_ge(S["fill%d" % t], n_fill[t])
+    def window_ready(q, t):
+        q.wait_ge(S["fill%d" % t], t)
         if t == 1:
             q.wait_ge(S.ul, 2)
         if t == 2:
@@ -147,22 +153,22 @@ def rank_program(g, core, T, topo):
         if t == 3:
             q.wait_ge(S.cp13, n_cp)
             q.wait_ge(S.cp23, n_cp)
-        q.wait_ge(S["%s%d" % (arrived, t)], need)
 
-    SY.dma_start(T.xt[:, :], T.x[:, :]).then_inc(S.ldx, 16)
+    SY.dma_start(T.xt[:, 0:2 * TL], T.x[:, 0:2 * TL]).then_inc(S.ldx0, 16)
     load_list(SY, T.sni, T.sn, range(0, 3), S.ldsn)
+    SY.dma_start(T.xt[:, 2 * TL:4 * TL], T.x[:, 2 * TL:4 * TL]).then_inc(S.ldx1, 16)
     SY.dma_start(T.wlt[:, :], T.wl[:, :]).then_inc(S.ldwl, 16)
     load_list(SY, T.lci, T.lc, range(8), S.ldls)
     load_list(SY, T.rci, T.rc, range(8), S.ldls)
-    SY.wait_ge(S.arc1, need_c)
-    SY.wait_ge(S.ars1, need_p)
+    SY.wait_ge(S.arc1, need(1, "c"))
+    SY.wait_ge(S.ars1, need(1, "s"))
     copy_slots(1, 1, 2, "cp12")
-    SY.wait_ge(S.goc2, sent_c)
-    SY.wait_ge(S.gos2, sent_p)
+    SY.wait_ge(S.goc2, sent(2, "c"))
+    SY.wait_ge(S.gos2, sent(2, "s"))
     copy_slots(1, 1, 3, "cp13")
     SY.dma_start(T.vt[:, :], T.v[:, :]).then_inc(S.ldv, 16)
-    SY.wait_ge(S.arc2, need_c)
-    SY.wait_ge(S.ars2, need_p)
+    SY.wait_ge(S.arc2, need(2, "c"))
+    SY.wait_ge(S.ars2, need(2, "s"))
     copy_slots(2, 2, 3, "cp23")
     SY.wait_ge(S.ycp, 1)
     SY.dma_start(T.y[:, :], T.yt[:, :]).then_inc(S.yst, 16)
@@ -171,40 +177,51 @@ def rank_program(g, core, T, topo):
     load_list(A, T.sni, T.sn, range(3, 8), S.ldsn)
     A.dma_start(T.wrt[:, :], T.wr[:, :]).then_inc(S.ldwr, 16)
     A.wait_ge(S.us1, n_us)
-    A.wait_ge(S.qx0, 1)
-    pick_plane("out1s", "w0s", WIDE[0], T.snu1, 0, (N - 1) * KS, S.ps1)
+    A.wait_ge(S.qx0, 2)
+    pick_to_send(A, 1)
     for t in (1, 2, 3):
-        window_ready(A, t, "ars", need_p)
-        pick_plane("a%ds" % t, "w%ds" % t, WIDE[t], T.lcu, KP * (t - 1), KP * t, S["als%d" % t])
-        pick_plane("b%ds" % t, "w%ds" % t, WIDE[t], T.rcu, KP * (t - 1), KP * t, S["bls%d" % t])
+        e0, e1 = KP * (t - 1), KP * t
+        eh = (e0 + e1) // 2
+        window_ready(A, t)
+        A.wait_ge(S["ars%d" % t], need(t, "s"))
+        pick_plane(A, "a%ds" % t, "w%ds" % t, WIDE[t], T.lcu, 0, e0, eh, S["als%d" % t])
+        pick_plane(A, "b%ds" % t, "w%ds" % t, WIDE[t], T.rcu, 0, e0, e1, S["bls%d" % t])
         scaled(A, t, 0)
         scaled(A, t, 2)
         if t < 3:
             A.wait_ge(S["us%d" % (t + 1)], n_us)
             A.wait_ge(S["qn%d" % t], 1)
-            pick_plane("out%ds" % (t + 1), "w%ds" % t, WIDE[t], T["snu%d" % (t + 1)], 0, (N - 1) * KS, S["ps%d" % (t + 1)])
+            pick_to_send(A, t + 1)
 
+    V.wait_ge(S.ldx0, 16)
+    quant("w0c", "w0s", 0, T.xt, TL // 2, S.qx0)
     V.wait_ge(S.ldsn, 128)
     list_to_send(1)
-    V.wait_ge(S.ldx, 16)
-    quant("w0c", "w0s", 0, T.xt, TL, S.qx0)
+    V.wait_ge(S.ldx1, 16)
+    quant("w0c", "w0s", TL // 2, T.xt, TL // 2, S.qx0, TL // 2)
     V.wait_ge(S.us1, n_us)
-    V.wait_ge(S.qx0, 1)
-    pick_codes("out1c", "w0c", WIDE[0], T.snu1, 0, (N - 1) * KS, S.pc1)
+    V.wait_ge(S.qx0, 2)
+    pick_to_send(V, 1)
     quant("w1c", "w1s", 0, T.xt, TL, S.fill1)
-    list_to_send(2)
-    list_to_send(3)
+    V.wait_ge(S.ldwl, 16)
+    quant("wlc", "wls", 0, T.wlt, 512, S.qwl)
     V.wait_ge(S.ldls, 256)
     V.tensor_copy(T.lcu[:, :], T.lci[:, :]).then_inc(S.ul, 1)
     V.tensor_copy(T.rcu[:, :], T.rci[:, :]).then_inc(S.ul, 1)
-    V.wait_ge(S.ldwl, 16)
-    quant("wlc", "wls", 0, T.wlt, 512, S.qwl)
     V.wait_ge(S.ldwr, 16)
     quant("wrc", "wrs", 0, T.wrt, 512, S.qwr)
     for t in (1, 2, 3):
-        window_ready(V, t, "arc", need_c)
-        pick_codes("a%dc" % t, "w%dc" % t, WIDE[t], T.lcu, KP * (t - 1), KP * t, S["alc%d" % t])
-        pick_codes("b%dc" % t, "w%dc" % t, WIDE[t], T.rcu, KP * (t - 1), KP * t, S["blc%d" % t])
+        e0, e1 = KP * (t - 1), KP * t
+        eh = (e0 + e1) // 2
+        window_ready(V, t)
+        V.wait_ge(S["arc%d" % t], need(t, "c"))
+        pick_codes("a%dc" % t, "w%dc" % t, WIDE[t], T.lcu, 0, e0, eh, S["alc%d" % t])
+        pick_codes("a%dc" % t, "w%dc" % t, WIDE[t], T.lcu, eh - e0, eh, e1, S["alc%d" % t])
+        V.wait_ge(S["ars%d" % t], need(t, "s"))
+        pick_plane(V, "a%ds" % t, "w%ds" % t, WIDE[t], T.lcu, eh - e0, eh, e1, S["als%d" % t])
+        pick_codes("b%dc" % t, "w%dc" % t, WIDE[t], T.rcu, 0, e0, e1, S["blc%d" % t])
+        if t < 3:
+            list_to_send(t + 1)
         scaled(V, t, 1)
         scaled(V, t, 3)
         V.wait_ge(S["ev%d" % t], 4)
@@ -212,7 +229,7 @@ def rank_program(g, core, T, topo):
             quant("w%dc" % t, "w%ds" % t, TL + (t - 1) * P, T["h%d" % t], P, S["qn%d" % t])
             V.wait_ge(S["us%d" % (t + 1)], n_us)
             V.wait_ge(S["qn%d" % t], 1)
-            pick_codes("out%dc" % (t + 1), "w%dc" % t, WIDE[t], T["snu%d" % (t + 1)], 0, (N - 1) * KS, S["pc%d" % (t + 1)])
+            pick_to_send(V, t + 1)
             u = t + 1
             quant("w%dc" % u, "w%ds" % u, 0, T.xt, TL, S["fill%d" % u])
             for k in range(1, u):
@@ -226,10 +243,10 @@ def rank_program(g, core, T, topo):
     V.tensor_copy(T.yt[:, :], T.acc[:, bank(2, 0):bank(2, 0) + P]).then_inc(S.ycp, 1)
 
     for t in (1, 2, 3):
-        for w, k, q in (("wl", "a", S.qwl), ("wr", "b", S.qwr)):
+        for w, k, q, n in (("wl", "a", S.qwl, 2), ("wr", "b", S.qwr, 1)):
             PE.wait_ge(q, 1)
-            PE.wait_ge(S["%slc%d" % (k, t)], 1)
-            PE.wait_ge(S["%sls%d" % (k, t)], 1)
+            PE.wait_ge(S["%slc%d" % (k, t)], n)
+            PE.wait_ge(S["%sls%d" % (k, t)], n)
             for i in range(4):
                 m = PE.matmul_mx(T.acc[:, bank(t, i):bank(t, i) + P],
                                  T[w + "c"][:, 128 * i:128 * i + 128], T[w + "s"][:, 128 * i:128 * i + 128],
@@ -243,5 +260,5 @@ def rank_program(g, core, T, topo):
     for t in (1, 2, 3):
         send(t)
     for t in (1, 2, 3):
-        g.wait_ge(S["goc%d" % t], sent_c)
-        g.wait_ge(S["gos%d" % t], sent_p)
+        g.wait_ge(S["goc%d" % t], sent(t, "c"))
+        g.wait_ge(S["gos%d" % t], sent(t, "s"))

from concourse.mybir import dt, AluOpType, ActivationFunctionType

N, TL, P, CAPP = 4, 256, 128, 32
BASE = TL + 3 * P
KP = P // 16
KS = CAPP // 16
CODES, PLANE = "float8_e4m3fn_x4", "uint8"
WIDE = [TL, BASE + N * CAPP, BASE + 2 * N * CAPP, BASE + 3 * N * CAPP]
FIRST = {"c": ((0, 2), (2, 4), (4, 6)), "s": ((6, 8), (0, 4), (4, 8))}

SCRATCH = {
    "xt": ("sbuf", [128, 4 * TL], "bfloat16"),
    "wlt": ("sbuf", [128, 2048], "bfloat16"),
    "wrt": ("sbuf", [128, 2048], "bfloat16"),
    "vt": ("sbuf", [128, 512], "bfloat16"),
    "sni": ("sbuf", [128, 3 * N * KS], "int32"),
    "lci": ("sbuf", [128, 3 * KP], "int32"),
    "rci": ("sbuf", [128, 3 * KP], "int32"),
    "lcu": ("sbuf", [128, 3 * KP], "uint16"),
    "rcu": ("sbuf", [128, 3 * KP], "uint16"),
    "wlc": ("sbuf", [128, 512], CODES), "wls": ("sbuf", [128, 512], PLANE),
    "wrc": ("sbuf", [128, 512], CODES), "wrs": ("sbuf", [128, 512], PLANE),
    "vc": ("sbuf", [128, 128], CODES), "vs": ("sbuf", [128, 128], PLANE),
    "hc": ("sbuf", [128, P], CODES), "hs": ("sbuf", [128, P], PLANE),
    "yt": ("sbuf", [128, P], "float32"),
    "acc": ("psum", [128, 512 * 8], "float32"),
}
for _t in range(4):
    SCRATCH["w%dc" % _t] = ("sbuf", [128, WIDE[_t]], CODES)
    SCRATCH["w%ds" % _t] = ("sbuf", [128, WIDE[_t]], PLANE)
for _t in (1, 2, 3):
    SCRATCH["snu%d" % _t] = ("sbuf", [128, (N - 1) * KS], "uint16")
    SCRATCH["out%dc" % _t] = ("sbuf", [128, (N - 1) * CAPP], CODES)
    SCRATCH["out%ds" % _t] = ("sbuf", [128, (N - 1) * CAPP], PLANE)
    SCRATCH["a%dc" % _t] = ("sbuf", [128, P], CODES)
    SCRATCH["a%ds" % _t] = ("sbuf", [128, P], PLANE)
    SCRATCH["b%dc" % _t] = ("sbuf", [128, P], CODES)
    SCRATCH["b%ds" % _t] = ("sbuf", [128, P], PLANE)
    SCRATCH["h%d" % _t] = ("sbuf", [128, 4 * P], "bfloat16")

SEMAPHORES = ["ldx0", "ldx1", "ldsn", "ldwl", "ldwr", "ldls", "ldv", "qx0", "ul", "qwl", "qwr", "qv", "qh", "ymm", "ycp",
              "yst", "fill1", "fill2", "fill3", "cp12", "cp13", "cp23"]
for _t in (1, 2, 3):
    SEMAPHORES += ["%s%d" % (_n, _t) for _n in ("us", "pcf", "pcr", "psf", "psr", "goc", "gos", "arc", "ars",
                                               "alc", "als", "blc", "bls", "ev", "qn", "m0x", "m1x", "m2x", "m3x")]


def rank_program(g, core, T, topo):
    me = T.rank_of(core)
    if me is None:
        return
    S, V, A, PE, SY = T.sem, g.vector, g.scalar, g.tensor, g.sync
    COPY, RELU = ActivationFunctionType.Copy, ActivationFunctionType.Relu

    def receivers(s):
        return [(s + 1 + j) % N for j in range(N - 1)]

    def lanes(s, d, t, kind):
        e = topo.engines(T.cores[s], T.cores[d])
        if t > 1:
            return e
        a, b = FIRST[kind][receivers(s).index(d)]
        return e[a * len(e) // 8:b * len(e) // 8]

    def need(t, kind):
        return sum(len(lanes(s, me, t, kind)) for s in range(N) if s != me)

    def sent(t, kind):
        return sum(len(lanes(me, d, t, kind)) for d in receivers(me))

    def slot(t, s):
        return BASE + ((t - 1) * N + s) * CAPP

    runs = [(a, b) for a, b in ((0, me), (me + 1, N)) if a < b]

    def load_list(q, dst, src, groups, sem):
        for k in groups:
            q.dma_start(dst[16 * k:16 * k + 16, :], src[:, :]).then_inc(sem, 16)

    def quant(wc, ws, col, tile, n, sem, at=0):
        V.quantize_mx(T[wc][:, col:col + n], T[ws][:, col:col + n], tile[:, 4 * at:4 * (at + n)]).then_inc(sem, 1)

    def pick_codes(out, win, wide, off, o0, e0, e1, sem):
        V.tensor_copy(T[out][:, 16 * o0:16 * (o0 + e1 - e0)].bitcast(dt.uint32),
                      T[win][:, 0:wide].bitcast(dt.uint32).indirect(off[:, e0:e1])).then_inc(sem, 1)

    def pick_plane(q, out, win, wide, off, o0, e0, e1, sem):
        dst, src = T[out][:, 16 * o0:16 * (o0 + e1 - e0)], T[win][:, 0:wide].indirect(off[:, e0:e1])
        if q is A:
            A.activation(dst, src, COPY).then_inc(sem, 1)
        else:
            V.tensor_copy(dst, src).then_inc(sem, 1)

    def list_to_send(t):
        c0 = (t - 1) * N * KS
        first = (me + 1) % N
        parts = [(first * KS, N * KS)] if first else []
        if me:
            parts.append((0, me * KS))
        at = 0
        for a, b in parts:
            V.tensor_copy(T["snu%d" % t][:, at:at + b - a], T.sni[:, c0 + a:c0 + b]).then_inc(S["us%d" % t], 1)
            at += b - a
    n_us = 1 if me in (0, N - 1) else 2

    def pick_to_send(q, t):
        w, off = t - 1, T["snu%d" % t]
        for e0, e1, f in ((0, KS, "f"), (KS, (N - 1) * KS, "r")):
            if q is V:
                pick_codes("out%dc" % t, "w%dc" % w, WIDE[w], off, e0, e0, e1, S["pc%s%d" % (f, t)])
            else:
                pick_plane(A, "out%ds" % t, "w%ds" % w, WIDE[w], off, e0, e0, e1, S["ps%s%d" % (f, t)])

    def send(t):
        for kind, left, arrive in (("c", "goc", "arc"), ("s", "gos", "ars")):
            for j, d in enumerate(receivers(me)):
                if j < 2:
                    g.wait_ge(S["p%s%s%d" % (kind, "fr"[j], t)], 1)
                rid, pid, _se = topo.addr(T.cores[d])
                src = T["out%d%s" % (t, kind)][:, CAPP * j:CAPP * j + CAPP]
                dst = T["w%d%s" % (t, kind)][:, slot(t, me):slot(t, me) + CAPP]
                if kind == "c":
                    src, dst = src.bitcast(dt.uint8), dst.bitcast(dt.uint8)
                mask = 0
                for e in lanes(me, d, t, kind):
                    mask |= 1 << e
                g.remote_dma(dst, src, S["%s%d" % (arrive, t)], S["%s%d" % (left, t)], pid, rid, mask)

    def copy_slots(t, src, dst, sem):
        for a, b in runs:
            c0, c1 = slot(t, a), slot(t, b)
            SY.dma_start(T["w%dc" % dst][:, c0:c1].bitcast(dt.uint8), T["w%dc" % src][:, c0:c1].bitcast(dt.uint8)).then_inc(S[sem], 16)
            SY.dma_start(T["w%ds" % dst][:, c0:c1], T["w%ds" % src][:, c0:c1]).then_inc(S[sem], 16)
    n_cp = 32 * len(runs)

    def bank(t, i):
        return 512 * (4 * ((t - 1) % 2) + i)

    def scaled(q, t, i):
        q.wait_ge(S["m%dx%d" % (i, t)], 1)
        out, z = T["h%d" % t][:, i:4 * P:4], T.acc[:, bank(t, i):bank(t, i) + P]
        if q is A:
            A.activation(out, z, RELU, scale=0.05).then_inc(S["ev%d" % t], 1)
        else:
            V.tensor_scalar(out, z, 0.0, 0.05, AluOpType.max, AluOpType.mult).then_inc(S["ev%d" % t], 1)

    def window_ready(q, t):
        q.wait_ge(S["fill%d" % t], t)
        if t == 1:
            q.wait_ge(S.ul, 2)
        if t == 2:
            q.wait_ge(S.cp12, n_cp)
        if t == 3:
            q.wait_ge(S.cp13, n_cp)
            q.wait_ge(S.cp23, n_cp)

    SY.dma_start(T.xt[:, 0:2 * TL], T.x[:, 0:2 * TL]).then_inc(S.ldx0, 16)
    load_list(SY, T.sni, T.sn, range(0, 3), S.ldsn)
    SY.dma_start(T.xt[:, 2 * TL:4 * TL], T.x[:, 2 * TL:4 * TL]).then_inc(S.ldx1, 16)
    SY.dma_start(T.wlt[:, :], T.wl[:, :]).then_inc(S.ldwl, 16)
    load_list(SY, T.lci, T.lc, range(8), S.ldls)
    load_list(SY, T.rci, T.rc, range(8), S.ldls)
    SY.wait_ge(S.arc1, need(1, "c"))
    SY.wait_ge(S.ars1, need(1, "s"))
    copy_slots(1, 1, 2, "cp12")
    SY.wait_ge(S.goc2, sent(2, "c"))
    SY.wait_ge(S.gos2, sent(2, "s"))
    copy_slots(1, 1, 3, "cp13")
    SY.dma_start(T.vt[:, :], T.v[:, :]).then_inc(S.ldv, 16)
    SY.wait_ge(S.arc2, need(2, "c"))
    SY.wait_ge(S.ars2, need(2, "s"))
    copy_slots(2, 2, 3, "cp23")
    SY.wait_ge(S.ycp, 1)
    SY.dma_start(T.y[:, :], T.yt[:, :]).then_inc(S.yst, 16)
    SY.wait_ge(S.yst, 16)

    load_list(A, T.sni, T.sn, range(3, 8), S.ldsn)
    A.dma_start(T.wrt[:, :], T.wr[:, :]).then_inc(S.ldwr, 16)
    A.wait_ge(S.us1, n_us)
    A.wait_ge(S.qx0, 2)
    pick_to_send(A, 1)
    for t in (1, 2, 3):
        e0, e1 = KP * (t - 1), KP * t
        eh = (e0 + e1) // 2
        window_ready(A, t)
        A.wait_ge(S["ars%d" % t], need(t, "s"))
        pick_plane(A, "a%ds" % t, "w%ds" % t, WIDE[t], T.lcu, 0, e0, eh, S["als%d" % t])
        pick_plane(A, "b%ds" % t, "w%ds" % t, WIDE[t], T.rcu, 0, e0, e1, S["bls%d" % t])
        scaled(A, t, 0)
        scaled(A, t, 2)
        if t < 3:
            A.wait_ge(S["us%d" % (t + 1)], n_us)
            A.wait_ge(S["qn%d" % t], 1)
            pick_to_send(A, t + 1)

    V.wait_ge(S.ldx0, 16)
    quant("w0c", "w0s", 0, T.xt, TL // 2, S.qx0)
    V.wait_ge(S.ldsn, 128)
    list_to_send(1)
    V.wait_ge(S.ldx1, 16)
    quant("w0c", "w0s", TL // 2, T.xt, TL // 2, S.qx0, TL // 2)
    V.wait_ge(S.us1, n_us)
    V.wait_ge(S.qx0, 2)
    pick_to_send(V, 1)
    quant("w1c", "w1s", 0, T.xt, TL, S.fill1)
    V.wait_ge(S.ldwl, 16)
    quant("wlc", "wls", 0, T.wlt, 512, S.qwl)
    V.wait_ge(S.ldls, 256)
    V.tensor_copy(T.lcu[:, :], T.lci[:, :]).then_inc(S.ul, 1)
    V.tensor_copy(T.rcu[:, :], T.rci[:, :]).then_inc(S.ul, 1)
    V.wait_ge(S.ldwr, 16)
    quant("wrc", "wrs", 0, T.wrt, 512, S.qwr)
    for t in (1, 2, 3):
        e0, e1 = KP * (t - 1), KP * t
        eh = (e0 + e1) // 2
        window_ready(V, t)
        V.wait_ge(S["arc%d" % t], need(t, "c"))
        pick_codes("a%dc" % t, "w%dc" % t, WIDE[t], T.lcu, 0, e0, eh, S["alc%d" % t])
        pick_codes("a%dc" % t, "w%dc" % t, WIDE[t], T.lcu, eh - e0, eh, e1, S["alc%d" % t])
        V.wait_ge(S["ars%d" % t], need(t, "s"))
        pick_plane(V, "a%ds" % t, "w%ds" % t, WIDE[t], T.lcu, eh - e0, eh, e1, S["als%d" % t])
        pick_codes("b%dc" % t, "w%dc" % t, WIDE[t], T.rcu, 0, e0, e1, S["blc%d" % t])
        if t < 3:
            list_to_send(t + 1)
        scaled(V, t, 1)
        scaled(V, t, 3)
        V.wait_ge(S["ev%d" % t], 4)
        if t < 3:
            quant("w%dc" % t, "w%ds" % t, TL + (t - 1) * P, T["h%d" % t], P, S["qn%d" % t])
            V.wait_ge(S["us%d" % (t + 1)], n_us)
            V.wait_ge(S["qn%d" % t], 1)
            pick_to_send(V, t + 1)
            u = t + 1
            quant("w%dc" % u, "w%ds" % u, 0, T.xt, TL, S["fill%d" % u])
            for k in range(1, u):
                quant("w%dc" % u, "w%ds" % u, TL + (k - 1) * P, T["h%d" % k], P, S["fill%d" % u])
        else:
            quant("hc", "hs", 0, T.h3, P, S.qh)
        if t == 2:
            V.wait_ge(S.ldv, 16)
            quant("vc", "vs", 0, T.vt, 128, S.qv)
    V.wait_ge(S.ymm, 1)
    V.tensor_copy(T.yt[:, :], T.acc[:, bank(2, 0):bank(2, 0) + P]).then_inc(S.ycp, 1)

    for t in (1, 2, 3):
        for w, k, q, n in (("wl", "a", S.qwl, 2), ("wr", "b", S.qwr, 1)):
            PE.wait_ge(q, 1)
            PE.wait_ge(S["%slc%d" % (k, t)], n)
            PE.wait_ge(S["%sls%d" % (k, t)], n)
            for i in range(4):
                m = PE.matmul_mx(T.acc[:, bank(t, i):bank(t, i) + P],
                                 T[w + "c"][:, 128 * i:128 * i + 128], T[w + "s"][:, 128 * i:128 * i + 128],
                                 T["%s%dc" % (k, t)][:, :], T["%s%ds" % (k, t)][:, :], k == "a", k == "b")
                if k == "b":
                    m.then_inc(S["m%dx%d" % (i, t)], 1)
    PE.wait_ge(S.qv, 1)
    PE.wait_ge(S.qh, 1)
    PE.matmul_mx(T.acc[:, bank(2, 0):bank(2, 0) + P], T.vc[:, :], T.vs[:, :], T.hc[:, :], T.hs[:, :], True, True).then_inc(S.ymm, 1)

    for t in (1, 2, 3):
        send(t)
    for t in (1, 2, 3):
        g.wait_ge(S["goc%d" % t], sent(t, "c"))
        g.wait_ge(S["gos%d" % t], sent(t, "s"))
